import numpy as np, ml_dtypes
CORES = [16,23,24,31,64,71]
N = 6
C = 1024
def setup_inputs(rng):
    return {"x": rng.standard_normal((N, 128, C), dtype=np.float32).astype(ml_dtypes.bfloat16)}
def setup_inputs_big(rng):
    d = setup_inputs(rng)
    for k in ("x",): d[k] = (d[k].astype(np.float32) * 1048576.0).astype(d[k].dtype)
    return d
def setup_inputs_small(rng):
    d = setup_inputs(rng)
    for k in ("x",): d[k] = (d[k].astype(np.float32) * (1 / 1048576.0)).astype(d[k].dtype)
    return d
def setup_inputs_apart(rng):
    d = setup_inputs(rng)
    f = (10.0 ** rng.permutation(np.linspace(-1.5, 1.5, N))).astype(np.float32).reshape(N, 1, 1)
    for k in ("x",): d[k] = (d[k].astype(np.float32) * f).astype(d[k].dtype)
    return d
def reference(x):
    X = x.astype(np.float64)
    y = np.stack([sum(np.maximum(X[r] - X[s], 0.0) for s in range(N)) for r in range(N)])
    return {"y": y.astype(ml_dtypes.bfloat16)}

@@ -1,0 +1,296 @@
+from concourse.bass import DstId, RemoteDMATransfer
+from concourse.mybir import AluOpType
+
+NSIM = 80
+C = 1024
+WMAX = 192
+WIDTH = {1: 192, 2: 128}
+ON_CAP = 4
+YL0 = 256
+
+SCRATCH = {
+    "xs": ("sbuf", [128, C], "bfloat16"),
+    "yl": ("sbuf", [128, C], "bfloat16"),
+    "xin": ("sbuf", [128, 6 * WMAX], "bfloat16"),
+    "rl": ("sbuf", [128, 2 * WMAX], "bfloat16"),
+    "nb": ("sbuf", [128, 15 * WMAX], "bfloat16"),
+    "yo": ("sbuf", [128, 6 * WMAX], "bfloat16"),
+    "zc": ("sbuf", [128, 385], "bfloat16"),
+    "cm": ("sbuf", [128, 384], "bfloat16"),
+    "dz": ("dram", [385, 128], "bfloat16"),
+    "xp0": ("psum", [128, 512], "float32"),
+    "xp1": ("psum", [128, 512], "float32"),
+    "xp2": ("psum", [128, 512], "float32"),
+    "ac0": ("psum", [128, 512], "float32"),
+    "ac1": ("psum", [128, 512], "float32"),
+    "ac2": ("psum", [128, 512], "float32"),
+    "ac3": ("psum", [128, 512], "float32"),
+    "ac4": ("psum", [128, 512], "float32"),
+}
+SEMAPHORES = ["ld", "st", "snt", "rarr", "yarr", "xa0", "xa1", "xa2", "xa3", "xa4", "xa5",
+              "cs", "cd1", "cd2", "pex", "pec", "pey", "v", "vy"]
+
+
+def _bits(mask):
+    return [e for e in range(mask.bit_length()) if (mask >> e) & 1]
+
+
+def _give(pool, n, cap):
+    per = 1
+    while per * 2 * n <= len(pool) and per * 2 <= cap:
+        per *= 2
+    return [sum(1 << e for e in pool[t * per:(t + 1) * per]) for t in range(n)], per
+
+
+def _call(topo, src, trs):
+    off = [t for t in trs if topo.chip(t[0]) != topo.chip(src)]
+    on = [t for t in trs if topo.chip(t[0]) == topo.chip(src)]
+    out = []
+    far = []
+    if off:
+        far = _bits(topo.mask(src, off[0][0]))
+        masks, per = _give(far, len(off), len(far))
+        out += [(t, m, per) for t, m in zip(off, masks)]
+    if on:
+        every = _bits(topo.mask(src, on[0][0]))
+        some_far = [c for c in range(NSIM) if topo.chip(c) != topo.chip(src) and topo.may_write(src, c)]
+        can_leave = _bits(topo.mask(src, some_far[0]))
+        pool = [e for e in every if e not in can_leave] + [e for e in every if e in can_leave and e not in far]
+        masks, per = _give(pool, len(on), ON_CAP)
+        out += [(t, m, per) for t, m in zip(on, masks)]
+    return out
+
+
+def _by_width(trs):
+    ws = sorted({t[5] for t in trs}, reverse=True)
+    return [[t for t in trs if t[5] == w] for w in ws]
+
+
+def _plan(T, topo):
+    ranks = list(T.cores)
+    chips = sorted({topo.chip(c) for c in ranks})
+
+    def on_chip(ch):
+        return [c for c in range(NSIM) if topo.chip(c) == ch]
+
+    comp = []
+    for ch in chips:
+        for d in sorted({topo.die(c) for c in on_chip(ch)}):
+            cand = [c for c in on_chip(ch) if topo.die(c) == d and all(c == r or topo.may_write(c, r) for r in ranks)]
+            comp.append(min(cand, key=lambda c: (c not in ranks, c)))
+    comp.sort()
+    late = {cc: [r for r in ranks if r != cc and not topo.may_write(r, cc)] for cc in comp}
+    shard = {}
+    c0 = 0
+    for cc in comp:
+        shard[cc] = (c0, WIDTH[len(late[cc])])
+        c0 += shard[cc][1]
+    assert c0 == C
+
+    scatter = {r: [] for r in ranks}
+    relay = {}
+    for ri, r in enumerate(ranks):
+        first, direct, load = [], [], {}
+        for cc in comp:
+            s0, w = shard[cc]
+            if cc == r:
+                continue
+            if topo.may_write(r, cc):
+                direct.append((cc, "xs", s0, "xin", ri * WMAX, w, "xa%d" % ri))
+                continue
+            cand = [c for c in on_chip(topo.chip(r))
+                    if c not in ranks and topo.may_write(c, cc) and topo.die(c) == topo.die(cc)]
+            q = min(cand, key=lambda c: (load.get(c, 0), c not in comp, c))
+            load[q] = load.get(q, 0) + 1
+            slot = len(relay.setdefault(q, []))
+            first.append((q, "xs", s0, "rl", slot * WMAX, w, "rarr"))
+            relay[q].append((cc, "rl", slot * WMAX, "xin", ri * WMAX, w, "xa%d" % ri))
+        scatter[r] = _by_width(first) + _by_width(direct)
+
+    calls = {}
+    for r in ranks:
+        calls.setdefault(r, []).extend(("scatter", _call(topo, r, trs)) for trs in scatter[r])
+    for q, trs in relay.items():
+        calls.setdefault(q, []).extend(("relay", _call(topo, q, grp)) for grp in _by_width(trs))
+
+    how = {}
+    for src, lst in calls.items():
+        for ci, (_, call) in enumerate(lst):
+            for t, m, per in call:
+                how[(t[0], t[6])] = (-per, ci)
+    order = {}
+    for cc in comp:
+        order[cc] = sorted(range(len(ranks)), key=lambda ri: (
+            ranks[ri] in late[cc], topo.chip(ranks[ri]) != topo.chip(cc), ranks[ri] != cc,
+            how.get((cc, "xa%d" % ri), (0, 0)), ri))
+
+    finals = {}
+    for cc in comp:
+        s0, w = shard[cc]
+        far = [ri for ri in order[cc][:5] if topo.chip(ranks[ri]) != topo.chip(cc)] + [order[cc][5]]
+        near = [ri for ri in order[cc][:5] if topo.chip(ranks[ri]) == topo.chip(cc) and ranks[ri] != cc]
+        own = [ri for ri in order[cc][:5] if ranks[ri] == cc]
+        finals[cc] = (far, near, own)
+        for name, grp in (("far", far), ("near", near)):
+            trs = [(ranks[ri], "yo", ri * WMAX, "yl", s0, w, "yarr") for ri in grp]
+            calls.setdefault(cc, []).append((name, _call(topo, cc, trs)))
+
+    arrive = {}
+    sent = {}
+    for src, lst in calls.items():
+        for _, call in lst:
+            for t, m, per in call:
+                arrive[(t[0], t[6])] = arrive.get((t[0], t[6]), 0) + per
+                sent[src] = sent.get(src, 0) + per
+    return dict(ranks=ranks, comp=comp, shard=shard, order=order, calls=calls, finals=finals,
+                arrive=arrive, sent=sent, late=late)
+
+
+def _issue(g, T, topo, call):
+    trs = []
+    for t, m, per in call:
+        dst, sb, s0, db, d0, w, sem = t
+        rid, pid, _se = topo.addr(dst)
+        trs.append(RemoteDMATransfer(dst_ids=[DstId(rid=rid, pnc=pid)], dma_engine_mask=m, remote_sem=T.sem[sem],
+                                     src=T[sb][:, s0:s0 + w], dst=T[db][:, d0:d0 + w]))
+    g.remote_dma_fused(trs, local_sem=T.sem.snt)
+
+
+def _compute(g, core, T, P):
+    S = T.sem
+    ranks = P["ranks"]
+    s0, w = P["shard"][core]
+    order = P["order"][core]
+    far, near, own = P["finals"][core]
+    pe, ve = g.tensor, g.vector
+
+    edges = [(0, 1, 1.0), (1, 128, 0.0), (128, 129, -1.0), (129, 256, 0.0), (256, 257, 5.0), (257, 385, 0.0)]
+    for a, b, val in edges:
+        ve.memset(T.zc[:, a:b], val).then_inc(S.cs, 1)
+    g.scalar.wait_ge(S.cs, len(edges))
+    g.scalar.dma_start(T.dz[:, :], T.zc[:, :]).then_inc(S.cd1, 16)
+    g.scalar.wait_ge(S.cd1, 16)
+    g.scalar.dma_start(T.cm[:, :], T.dz[0:384, :]).then_inc(S.cd2, 16)
+    eye, neg, five = T.cm[:, 0:128], T.cm[:, 128:256], T.cm[:, 256:384]
+
+    def X(k):
+        ri = order[k]
+        if ranks[ri] == core:
+            return T.xs[:, s0:s0 + w]
+        return T.xin[:, ri * WMAX:ri * WMAX + w]
+
+    def wait_x(q, k):
+        ri = order[k]
+        if ranks[ri] == core:
+            q.wait_ge(S.ld, 16)
+        else:
+            q.wait_ge(S["xa%d" % ri], P["arrive"][(core, "xa%d" % ri)])
+
+    xpb = [T.xp0, T.xp1, T.xp2]
+    acb = [T.ac0, T.ac1, T.ac2, T.ac3, T.ac4]
+
+    def XP(i):
+        return xpb[i // 2][:, (i % 2) * WMAX:(i % 2) * WMAX + w]
+
+    def need_pex(i):
+        return min(5, (i // 2) * 2 + 2)
+
+    yL = T.xp2[:, YL0:YL0 + w]
+    pairs = [(i, k) for k in range(1, 5) for i in range(k)] + [(i, 5) for i in (4, 0, 1, 2, 3)]
+    pos = {p: n for n, p in enumerate(pairs)}
+
+    def NB(p):
+        return T.nb[:, pos[p] * WMAX:pos[p] * WMAX + w]
+
+    pe.wait_ge(S.cd2, 16)
+
+    def bring(k):
+        wait_x(pe, k)
+        pe.matmul(XP(k), eye, X(k), start=True, stop=True).then_inc(S.pex, 1)
+
+    def open_acc(k):
+        pe.matmul(acb[k][:, 0:w], five, X(k), start=True, stop=False)
+
+    def add_pairs(k):
+        for i in range(k):
+            pe.wait_ge(S.v, pos[(i, k)] + 1)
+            m = pe.matmul(acb[i][:, 0:w], neg, NB((i, k)), start=False, stop=(k == 4))
+            if k == 4:
+                m.then_inc(S.pec, 1)
+            m = pe.matmul(acb[k][:, 0:w], neg, NB((i, k)), start=False, stop=(k == 4 and i == 3))
+            if k == 4 and i == 3:
+                m.then_inc(S.pec, 1)
+
+    ne = min(6 - len(P["late"][core]), 5)
+    for k in range(ne):
+        bring(k)
+    for k in range(ne):
+        open_acc(k)
+    for k in range(1, ne):
+        add_pairs(k)
+    for k in range(ne, 5):
+        bring(k)
+        open_acc(k)
+        add_pairs(k)
+    wait_x(pe, 5)
+    pe.wait_ge(S.v, pos[(4, 5)] + 1)
+    pe.matmul(yL, five, X(5), start=True, stop=False)
+    for n, i in enumerate((4, 0, 1, 2, 3)):
+        pe.wait_ge(S.v, pos[(i, 5)] + 1)
+        m = pe.matmul(yL, neg, NB((i, 5)), start=False, stop=(n == 4))
+        if n == 4:
+            m.then_inc(S.pey, 1)
+
+    seen = -1
+    for (i, k) in pairs:
+        if k != seen:
+            wait_x(ve, k)
+            seen = k
+        ve.wait_ge(S.pex, need_pex(i))
+        ve.tensor_tensor(NB((i, k)), XP(i), X(k), AluOpType.min).then_inc(S.v, 1)
+    ve.wait_ge(S.v, len(pairs))
+    for ri in far + near + own:
+        out = T.yl[:, s0:s0 + w] if ranks[ri] == core else T.yo[:, ri * WMAX:ri * WMAX + w]
+        i = order.index(ri)
+        if i == 5:
+            ve.wait_ge(S.pey, 1)
+            ve.tensor_copy(out, yL).then_inc(S.vy, 1)
+        else:
+            ve.wait_ge(S.pec, i + 1)
+            ve.tensor_tensor(out, acb[i][:, 0:w], NB((i, 5)), AluOpType.subtract).then_inc(S.vy, 1)
+    ve.wait_ge(S.pec, 5)
+
+
+def rank_program(g, core, T, topo):
+    P = _plan(T, topo)
+    S = T.sem
+    ranks, comp = P["ranks"], P["comp"]
+    if core not in P["calls"]:
+        return
+    is_rank = core in ranks
+
+    if is_rank:
+        g.sync.dma_start(T.xs[:, :], T.x[:, :]).then_inc(S.ld, 16)
+    if core in comp:
+        _compute(g, core, T, P)
+
+    done = 0
+    for stage, call in P["calls"][core]:
+        if not call:
+            continue
+        if stage == "scatter":
+            g.wait_ge(S.ld, 16)
+        elif stage == "relay":
+            g.wait_ge(S.rarr, P["arrive"][(core, "rarr")])
+        else:
+            done += len(call)
+            g.wait_ge(S.vy, done)
+        _issue(g, T, topo, call)
+    g.wait_ge(S.snt, P["sent"][core])
+
+    if is_rank:
+        g.sync.wait_ge(S.yarr, P["arrive"][(core, "yarr")])
+        if core in comp:
+            g.sync.wait_ge(S.vy, 6)
+        g.sync.dma_start(T.y[:, :], T.yl[:, :]).then_inc(S.st, 16)
+        g.sync.wait_ge(S.st, 16)

@@ -3,8 +3,9 @@ from concourse.mybir import AluOpType
 
 NSIM = 80
 C = 1024
-WMAX = 192
-WIDTH = {1: 192, 2: 128}
+ND = 2
+WMAX = 96
+WIDTH = {1: 96, 2: 64}
 ON_CAP = 4
 YL0 = 256
 
@@ -12,7 +13,7 @@ SCRATCH = {
     "xs": ("sbuf", [128, C], "bfloat16"),
     "yl": ("sbuf", [128, C], "bfloat16"),
     "xin": ("sbuf", [128, 6 * WMAX], "bfloat16"),
-    "rl": ("sbuf", [128, 2 * WMAX], "bfloat16"),
+    "rl": ("sbuf", [128, 4 * WMAX], "bfloat16"),
     "nb": ("sbuf", [128, 15 * WMAX], "bfloat16"),
     "yo": ("sbuf", [128, 6 * WMAX], "bfloat16"),
     "zc": ("sbuf", [128, 385], "bfloat16"),
@@ -27,7 +28,8 @@ SCRATCH = {
     "ac3": ("psum", [128, 512], "float32"),
     "ac4": ("psum", [128, 512], "float32"),
 }
-SEMAPHORES = ["ld", "st", "snt", "rarr", "yarr", "xa0", "xa1", "xa2", "xa3", "xa4", "xa5",
+SEMAPHORES = ["lda", "ldb", "st", "st2", "snt", "rarr", "ya0", "ya1", "ya2", "ya3",
+              "xa0", "xa1", "xa2", "xa3", "xa4", "xa5",
               "cs", "cd1", "cd2", "pex", "pec", "pey", "v", "vy"]
 
 
@@ -69,6 +71,7 @@ def _by_width(trs):
 def _plan(T, topo):
     ranks = list(T.cores)
     chips = sorted({topo.chip(c) for c in ranks})
+    all_chips = sorted({topo.chip(c) for c in range(NSIM)})
 
     def on_chip(ch):
         return [c for c in range(NSIM) if topo.chip(c) == ch]
@@ -77,39 +80,111 @@ def _plan(T, topo):
     for ch in chips:
         for d in sorted({topo.die(c) for c in on_chip(ch)}):
             cand = [c for c in on_chip(ch) if topo.die(c) == d and all(c == r or topo.may_write(c, r) for r in ranks)]
-            comp.append(min(cand, key=lambda c: (c not in ranks, c)))
-    comp.sort()
-    late = {cc: [r for r in ranks if r != cc and not topo.may_write(r, cc)] for cc in comp}
+            comp += sorted(cand, key=lambda c: (c not in ranks, c))[:ND]
+    barred_at = {cc: [r for r in ranks if r != cc and not topo.may_write(r, cc)] for cc in comp}
+    comp.sort(key=lambda c: (len(barred_at[c]), topo.chip(c), topo.die(c), c))
     shard = {}
     c0 = 0
     for cc in comp:
-        shard[cc] = (c0, WIDTH[len(late[cc])])
+        shard[cc] = (c0, WIDTH[len(barred_at[cc])])
         c0 += shard[cc][1]
     assert c0 == C
+    kinds = []
+    for cc in comp:
+        if topo.chip(cc) not in kinds:
+            kinds.append(topo.chip(cc))
+    group = {cc: kinds.index(topo.chip(cc)) for cc in comp}
+    span = [(min(shard[cc][0] for cc in comp if group[cc] == n),
+             max(shard[cc][0] + shard[cc][1] for cc in comp if group[cc] == n)) for n in range(len(kinds))]
+    split = min(shard[cc][0] for cc in comp if shard[cc][1] != shard[comp[0]][1])
 
-    scatter = {r: [] for r in ranks}
-    relay = {}
-    for ri, r in enumerate(ranks):
-        first, direct, load = [], [], {}
-        for cc in comp:
-            s0, w = shard[cc]
-            if cc == r:
-                continue
-            if topo.may_write(r, cc):
-                direct.append((cc, "xs", s0, "xin", ri * WMAX, w, "xa%d" % ri))
-                continue
-            cand = [c for c in on_chip(topo.chip(r))
-                    if c not in ranks and topo.may_write(c, cc) and topo.die(c) == topo.die(cc)]
-            q = min(cand, key=lambda c: (load.get(c, 0), c not in comp, c))
-            load[q] = load.get(q, 0) + 1
-            slot = len(relay.setdefault(q, []))
-            first.append((q, "xs", s0, "rl", slot * WMAX, w, "rarr"))
-            relay[q].append((cc, "rl", slot * WMAX, "xin", ri * WMAX, w, "xa%d" % ri))
-        scatter[r] = _by_width(first) + _by_width(direct)
+    feeds = {r: [] for r in ranks}
+    now = {r: [] for r in ranks}
+    later = {r: [] for r in ranks}
+    relay, fill, asem, via, busy = {}, {}, {}, set(), {}
+
+    def straight(lst, ri, cc):
+        s0, w = shard[cc]
+        lst.append((cc, "xs", s0, "xin", ri * w, w, "xa%d" % ri))
+        asem[(cc, ri)] = "xa%d" % ri
+
+    def room(q, w):
+        o = fill.get(q, 0)
+        fill[q] = o + w
+        busy[q] = busy.get(q, 0) + 1
+        return o
+
+    def hand(ri, q, part):
+        s0 = shard[part[0]][0]
+        wt = sum(shard[cc][1] for cc in part)
+        assert shard[part[-1]][0] + shard[part[-1]][1] - s0 == wt
+        o = room(q, wt)
+        feeds[ranks[ri]].append((q, "xs", s0, "rl", o, wt, "rarr"))
+        for cc in part:
+            w = shard[cc][1]
+            relay.setdefault(q, []).append((cc, "rl", o + shard[cc][0] - s0, "xin", ri * w, w, "xa%d" % ri))
+            asem[(cc, ri)] = "xa%d" % ri
+            via.add((cc, ri))
+
+    def helpers(ch, part, src=None):
+        return sorted([c for c in on_chip(ch) if c not in ranks and topo.die(c) == topo.die(part[0])
+                       and all(topo.may_write(c, cc) for cc in part) and (src is None or topo.may_write(src, c))],
+                      key=lambda c: (busy.get(c, 0), c not in comp, c))
+
+    for ch in chips:
+        rs = [ri for ri, r in enumerate(ranks) if topo.chip(r) == ch]
+        cross = []
+        for X in chips:
+            tg = [cc for cc in comp if topo.chip(cc) == X]
+            if X == ch or all(topo.may_write(ranks[ri], tg[0]) for ri in rs):
+                for ri in rs:
+                    for cc in tg:
+                        if cc != ranks[ri]:
+                            straight(now[ranks[ri]], ri, cc)
+            else:
+                cross.append(X)
+        if len(cross) == 1:
+            assert rs == list(range(rs[0], rs[0] + len(rs)))
+            for cc in [c for c in comp if topo.chip(c) == cross[0]]:
+                s0, w = shard[cc]
+                q = helpers(ch, [cc])[0]
+                o = room(q, w * len(rs))
+                for n, ri in enumerate(rs):
+                    feeds[ranks[ri]].append((q, "xs", s0, "rl", o + n * w, w, "rarr"))
+                    asem[(cc, ri)] = "xa%d" % rs[0]
+                    via.add((cc, ri))
+                relay.setdefault(q, []).append((cc, "rl", o, "xin", rs[0] * w, w * len(rs), "xa%d" % rs[0]))
+        elif cross:
+            pending = []
+            for X in cross:
+                tg = [cc for cc in comp if topo.chip(cc) == X]
+                for d in sorted({topo.die(cc) for cc in tg}):
+                    part = [cc for cc in tg if topo.die(cc) == d]
+                    for ri in rs:
+                        r = ranks[ri]
+                        if not topo.may_write(r, part[0]):
+                            if topo.mates(ch, X):
+                                hand(ri, helpers(ch, part)[0], part)
+                            else:
+                                Z = [z for z in all_chips if topo.mates(z, X)][0]
+                                hand(ri, helpers(Z, part, r)[0], part)
+                        elif topo.mates(ch, X):
+                            for cc in part:
+                                straight(now[r], ri, cc)
+                        else:
+                            pending.append((ri, part))
+            for ri, part in pending:
+                free = [c for c in helpers(ch, part) if c not in busy]
+                if free:
+                    hand(ri, free[0], part)
+                else:
+                    for cc in part:
+                        straight(later[ranks[ri]], ri, cc)
 
     calls = {}
     for r in ranks:
-        calls.setdefault(r, []).extend(("scatter", _call(topo, r, trs)) for trs in scatter[r])
+        calls[r] = [("scatter", _call(topo, r, trs))
+                    for trs in _by_width(feeds[r]) + _by_width(now[r]) + _by_width(later[r])]
     for q, trs in relay.items():
         calls.setdefault(q, []).extend(("relay", _call(topo, q, grp)) for grp in _by_width(trs))
 
@@ -117,12 +192,13 @@ def _plan(T, topo):
     for src, lst in calls.items():
         for ci, (_, call) in enumerate(lst):
             for t, m, per in call:
-                how[(t[0], t[6])] = (-per, ci)
+                how[(t[0], t[6])] = (ci, -per)
     order = {}
     for cc in comp:
         order[cc] = sorted(range(len(ranks)), key=lambda ri: (
-            ranks[ri] in late[cc], topo.chip(ranks[ri]) != topo.chip(cc), ranks[ri] != cc,
-            how.get((cc, "xa%d" % ri), (0, 0)), ri))
+            (cc, ri) in via, topo.chip(ranks[ri]) != topo.chip(cc), ranks[ri] != cc,
+            how.get((cc, asem.get((cc, ri))), (0, 0)), ri))
+    nlate = {cc: len([ri for ri in range(len(ranks)) if (cc, ri) in via]) for cc in comp}
 
     finals = {}
     for cc in comp:
@@ -132,7 +208,7 @@ def _plan(T, topo):
         own = [ri for ri in order[cc][:5] if ranks[ri] == cc]
         finals[cc] = (far, near, own)
         for name, grp in (("far", far), ("near", near)):
-            trs = [(ranks[ri], "yo", ri * WMAX, "yl", s0, w, "yarr") for ri in grp]
+            trs = [(ranks[ri], "yo", ri * WMAX, "yl", s0, w, "ya%d" % group[cc]) for ri in grp]
             calls.setdefault(cc, []).append((name, _call(topo, cc, trs)))
 
     arrive = {}
@@ -142,8 +218,8 @@ def _plan(T, topo):
             for t, m, per in call:
                 arrive[(t[0], t[6])] = arrive.get((t[0], t[6]), 0) + per
                 sent[src] = sent.get(src, 0) + per
-    return dict(ranks=ranks, comp=comp, shard=shard, order=order, calls=calls, finals=finals,
-                arrive=arrive, sent=sent, late=late)
+    return dict(ranks=ranks, comp=comp, shard=shard, order=order, calls=calls, finals=finals, arrive=arrive,
+                sent=sent, nlate=nlate, asem=asem, group=group, span=span, split=split)
 
 
 def _issue(g, T, topo, call):
@@ -177,14 +253,15 @@ def _compute(g, core, T, P):
         ri = order[k]
         if ranks[ri] == core:
             return T.xs[:, s0:s0 + w]
-        return T.xin[:, ri * WMAX:ri * WMAX + w]
+        return T.xin[:, ri * w:ri * w + w]
 
     def wait_x(q, k):
         ri = order[k]
         if ranks[ri] == core:
-            q.wait_ge(S.ld, 16)
+            q.wait_ge(S.lda if s0 < P["split"] else S.ldb, 16)
         else:
-            q.wait_ge(S["xa%d" % ri], P["arrive"][(core, "xa%d" % ri)])
+            name = P["asem"][(core, ri)]
+            q.wait_ge(S[name], P["arrive"][(core, name)])
 
     xpb = [T.xp0, T.xp1, T.xp2]
     acb = [T.ac0, T.ac1, T.ac2, T.ac3, T.ac4]
@@ -221,7 +298,7 @@ def _compute(g, core, T, P):
             if k == 4 and i == 3:
                 m.then_inc(S.pec, 1)
 
-    ne = min(6 - len(P["late"][core]), 5)
+    ne = min(6 - P["nlate"][core], 5)
     for k in range(ne):
         bring(k)
     for k in range(ne):
@@ -269,8 +346,12 @@ def rank_program(g, core, T, topo):
         return
     is_rank = core in ranks
 
+    split = P["split"]
     if is_rank:
-        g.sync.dma_start(T.xs[:, :], T.x[:, :]).then_inc(S.ld, 16)
+        a_first = P["calls"][core][0][1][0][0][2] < split
+        qa, qb = (g.sync, g.scalar) if a_first else (g.scalar, g.sync)
+        qa.dma_start(T.xs[:, 0:split], T.x[:, 0:split]).then_inc(S.lda, 16)
+        qb.dma_start(T.xs[:, split:C], T.x[:, split:C]).then_inc(S.ldb, 16)
     if core in comp:
         _compute(g, core, T, P)
 
@@ -279,7 +360,7 @@ def rank_program(g, core, T, topo):
         if not call:
             continue
         if stage == "scatter":
-            g.wait_ge(S.ld, 16)
+            g.wait_ge(S.lda if call[0][0][2] < split else S.ldb, 16)
         elif stage == "relay":
             g.wait_ge(S.rarr, P["arrive"][(core, "rarr")])
         else:
@@ -289,8 +370,14 @@ def rank_program(g, core, T, topo):
     g.wait_ge(S.snt, P["sent"][core])
 
     if is_rank:
-        g.sync.wait_ge(S.yarr, P["arrive"][(core, "yarr")])
-        if core in comp:
-            g.sync.wait_ge(S.vy, 6)
-        g.sync.dma_start(T.y[:, :], T.yl[:, :]).then_inc(S.st, 16)
-        g.sync.wait_ge(S.st, 16)
+        spans = P["span"]
+        count = {"st": 0, "st2": 0}
+        for n, (a, b) in enumerate(spans):
+            q, sem = (g.sync, "st") if 2 * n < len(spans) else (g.scalar, "st2")
+            q.wait_ge(S["ya%d" % n], P["arrive"][(core, "ya%d" % n)])
+            if core in comp and P["group"][core] == n:
+                q.wait_ge(S.vy, 6)
+            q.dma_start(T.y[:, a:b], T.yl[:, a:b]).then_inc(S[sem], 16)
+            count[sem] += 16
+        g.sync.wait_ge(S.st, count["st"])
+        g.scalar.wait_ge(S.st2, count["st2"])

@@ -7,6 +7,8 @@ ND = 2
 WMAX = 96
 WIDTH = {1: 96, 2: 64}
 ON_CAP = 4
+FEED_CAP = 8
+DIAG = (1.0, -1.0, 5.0)
 YL0 = 256
 
 SCRATCH = {
@@ -16,9 +18,8 @@ SCRATCH = {
     "rl": ("sbuf", [128, 4 * WMAX], "bfloat16"),
     "nb": ("sbuf", [128, 15 * WMAX], "bfloat16"),
     "yo": ("sbuf", [128, 6 * WMAX], "bfloat16"),
-    "zc": ("sbuf", [128, 385], "bfloat16"),
+    "zc": ("sbuf", [128, 128], "bfloat16"),
     "cm": ("sbuf", [128, 384], "bfloat16"),
-    "dz": ("dram", [385, 128], "bfloat16"),
     "xp0": ("psum", [128, 512], "float32"),
     "xp1": ("psum", [128, 512], "float32"),
     "xp2": ("psum", [128, 512], "float32"),
@@ -30,7 +31,7 @@ SCRATCH = {
 }
 SEMAPHORES = ["lda", "ldb", "st", "st2", "snt", "rarr", "ya0", "ya1", "ya2", "ya3",
               "xa0", "xa1", "xa2", "xa3", "xa4", "xa5",
-              "cs", "cd1", "cd2", "pex", "pec", "pey", "v", "vy"]
+              "cs", "ca", "cd", "pex", "pec", "pey", "v", "vy"]
 
 
 def _bits(mask):
@@ -44,7 +45,7 @@ def _give(pool, n, cap):
     return [sum(1 << e for e in pool[t * per:(t + 1) * per]) for t in range(n)], per
 
 
-def _call(topo, src, trs):
+def _call(topo, src, trs, cap=ON_CAP):
     off = [t for t in trs if topo.chip(t[0]) != topo.chip(src)]
     on = [t for t in trs if topo.chip(t[0]) == topo.chip(src)]
     out = []
@@ -58,7 +59,7 @@ def _call(topo, src, trs):
         some_far = [c for c in range(NSIM) if topo.chip(c) != topo.chip(src) and topo.may_write(src, c)]
         can_leave = _bits(topo.mask(src, some_far[0]))
         pool = [e for e in every if e not in can_leave] + [e for e in every if e in can_leave and e not in far]
-        masks, per = _give(pool, len(on), ON_CAP)
+        masks, per = _give(pool, len(on), cap)
         out += [(t, m, per) for t, m in zip(on, masks)]
     return out
 
@@ -101,7 +102,7 @@ def _plan(T, topo):
     feeds = {r: [] for r in ranks}
     now = {r: [] for r in ranks}
     later = {r: [] for r in ranks}
-    relay, fill, asem, via, busy = {}, {}, {}, set(), {}
+    relay, fill, asem, via, busy, thru = {}, {}, {}, set(), {}, {}
 
     def straight(lst, ri, cc):
         s0, w = shard[cc]
@@ -125,6 +126,7 @@ def _plan(T, topo):
             relay.setdefault(q, []).append((cc, "rl", o + shard[cc][0] - s0, "xin", ri * w, w, "xa%d" % ri))
             asem[(cc, ri)] = "xa%d" % ri
             via.add((cc, ri))
+            thru[(cc, ri)] = q
 
     def helpers(ch, part, src=None):
         return sorted([c for c in on_chip(ch) if c not in ranks and topo.die(c) == topo.die(part[0])
@@ -153,6 +155,7 @@ def _plan(T, topo):
                     feeds[ranks[ri]].append((q, "xs", s0, "rl", o + n * w, w, "rarr"))
                     asem[(cc, ri)] = "xa%d" % rs[0]
                     via.add((cc, ri))
+                    thru[(cc, ri)] = q
                 relay.setdefault(q, []).append((cc, "rl", o, "xin", rs[0] * w, w * len(rs), "xa%d" % rs[0]))
         elif cross:
             pending = []
@@ -175,6 +178,8 @@ def _plan(T, topo):
                             pending.append((ri, part))
             for ri, part in pending:
                 free = [c for c in helpers(ch, part) if c not in busy]
+                for Z in [z for z in all_chips if topo.mates(z, topo.chip(part[0]))]:
+                    free += [c for c in helpers(Z, part, ranks[ri]) if c not in busy]
                 if free:
                     hand(ri, free[0], part)
                 else:
@@ -183,21 +188,23 @@ def _plan(T, topo):
 
     calls = {}
     for r in ranks:
-        calls[r] = [("scatter", _call(topo, r, trs))
-                    for trs in _by_width(feeds[r]) + _by_width(now[r]) + _by_width(later[r])]
+        calls[r] = [("scatter", _call(topo, r, trs, FEED_CAP)) for trs in _by_width(feeds[r])]
+        calls[r] += [("scatter", _call(topo, r, trs)) for trs in _by_width(now[r]) + _by_width(later[r])]
     for q, trs in relay.items():
         calls.setdefault(q, []).extend(("relay", _call(topo, q, grp)) for grp in _by_width(trs))
 
-    how = {}
+    how, fed = {}, {}
     for src, lst in calls.items():
         for ci, (_, call) in enumerate(lst):
             for t, m, per in call:
                 how[(t[0], t[6])] = (ci, -per)
+                if src in ranks and t[3] == "rl":
+                    fed[(src, t[0])] = -per
     order = {}
     for cc in comp:
         order[cc] = sorted(range(len(ranks)), key=lambda ri: (
             (cc, ri) in via, topo.chip(ranks[ri]) != topo.chip(cc), ranks[ri] != cc,
-            how.get((cc, asem.get((cc, ri))), (0, 0)), ri))
+            how.get((cc, asem.get((cc, ri))), (0, 0)), fed.get((ranks[ri], thru.get((cc, ri))), 0), ri))
     nlate = {cc: len([ri for ri in range(len(ranks)) if (cc, ri) in via]) for cc in comp}
 
     finals = {}
@@ -211,15 +218,39 @@ def _plan(T, topo):
             trs = [(ranks[ri], "yo", ri * WMAX, "yl", s0, w, "ya%d" % group[cc]) for ri in grp]
             calls.setdefault(cc, []).append((name, _call(topo, cc, trs)))
 
+    warm = {}
+    for ch in chips:
+        R = sorted([c for c in comp if topo.chip(c) == ch], key=lambda c: (c in ranks, c))
+        E = [c for c in sorted(calls) if c not in comp and
+             (topo.chip(c) == ch if c in ranks else topo.chip(calls[c][0][1][0][0][0]) == ch)]
+        E.sort(key=lambda c: (c not in ranks, c))
+        kind = {c: n % 3 for n, c in enumerate(R)}
+        kind.update({c: 1 + n % 2 for n, c in enumerate(E)})
+        gets = {c: [] for c in R + E}
+        for c in R:
+            for k in range(3):
+                if kind[c] != k:
+                    cand = [q for q in R + E if kind[q] == k and q != c and topo.may_write(q, c)]
+                    gets[min(cand, key=lambda q: (len(gets[q]), q in ranks, q))].append(c)
+        for q in R + E:
+            assert gets[q]
+            m = topo.mask(q, gets[q][0])
+            assert all(topo.mask(q, c) == m for c in gets[q])
+            warm[q] = (kind[q], gets[q], m, len(_bits(m)))
+
     arrive = {}
     sent = {}
+    for q, (k, ds, m, per) in warm.items():
+        sent[q] = per
+        for c in ds:
+            arrive[(c, "cd")] = arrive.get((c, "cd"), 0) + per
     for src, lst in calls.items():
         for _, call in lst:
             for t, m, per in call:
                 arrive[(t[0], t[6])] = arrive.get((t[0], t[6]), 0) + per
                 sent[src] = sent.get(src, 0) + per
     return dict(ranks=ranks, comp=comp, shard=shard, order=order, calls=calls, finals=finals, arrive=arrive,
-                sent=sent, nlate=nlate, asem=asem, group=group, span=span, split=split)
+                sent=sent, warm=warm, nlate=nlate, asem=asem, group=group, span=span, split=split, gchip=kinds)
 
 
 def _issue(g, T, topo, call):
@@ -240,13 +271,6 @@ def _compute(g, core, T, P):
     far, near, own = P["finals"][core]
     pe, ve = g.tensor, g.vector
 
-    edges = [(0, 1, 1.0), (1, 128, 0.0), (128, 129, -1.0), (129, 256, 0.0), (256, 257, 5.0), (257, 385, 0.0)]
-    for a, b, val in edges:
-        ve.memset(T.zc[:, a:b], val).then_inc(S.cs, 1)
-    g.scalar.wait_ge(S.cs, len(edges))
-    g.scalar.dma_start(T.dz[:, :], T.zc[:, :]).then_inc(S.cd1, 16)
-    g.scalar.wait_ge(S.cd1, 16)
-    g.scalar.dma_start(T.cm[:, :], T.dz[0:384, :]).then_inc(S.cd2, 16)
     eye, neg, five = T.cm[:, 0:128], T.cm[:, 128:256], T.cm[:, 256:384]
 
     def X(k):
@@ -279,7 +303,8 @@ def _compute(g, core, T, P):
     def NB(p):
         return T.nb[:, pos[p] * WMAX:pos[p] * WMAX + w]
 
-    pe.wait_ge(S.cd2, 16)
+    pe.wait_ge(S.ca, 1)
+    pe.wait_ge(S.cd, P["arrive"][(core, "cd")])
 
     def bring(k):
         wait_x(pe, k)
@@ -350,8 +375,22 @@ def rank_program(g, core, T, topo):
     if is_rank:
         a_first = P["calls"][core][0][1][0][0][2] < split
         qa, qb = (g.sync, g.scalar) if a_first else (g.scalar, g.sync)
-        qa.dma_start(T.xs[:, 0:split], T.x[:, 0:split]).then_inc(S.lda, 16)
-        qb.dma_start(T.xs[:, split:C], T.x[:, split:C]).then_inc(S.ldb, 16)
+        for first in (True, False):
+            if first == a_first:
+                qa.dma_start(T.xs[:, 0:split], T.x[:, 0:split]).then_inc(S.lda, 16)
+            else:
+                qb.dma_start(T.xs[:, split:C], T.x[:, split:C]).then_inc(S.ldb, 16)
+
+    k, takers, m, per = P["warm"][core]
+    part = T.cm[:, k * 128:(k + 1) * 128]
+    g.vector.memset(T.zc[:, :], DIAG[k]).then_inc(S.cs, 1)
+    g.wait_ge(S.cs, 1)
+    g.affine_select(part, T.zc[:, :], [[-1, 128]], AluOpType.is_equal, 0.0, 0, 1).then_inc(S.ca, 1)
+    g.wait_ge(S.ca, 1)
+    ids = [DstId(rid=topo.addr(c)[0], pnc=topo.addr(c)[1]) for c in takers]
+    g.remote_dma_fused([RemoteDMATransfer(dst_ids=ids, dma_engine_mask=m, remote_sem=S.cd, srcs=[part],
+                                          dsts=[part for c in takers])], local_sem=S.snt)
+
     if core in comp:
         _compute(g, core, T, P)
 
@@ -371,13 +410,16 @@ def rank_program(g, core, T, topo):
 
     if is_rank:
         spans = P["span"]
+        near = [n for n in range(len(spans)) if P["gchip"][n] == topo.chip(core)]
+        far = [n for n in range(len(spans)) if n not in near]
         count = {"st": 0, "st2": 0}
-        for n, (a, b) in enumerate(spans):
-            q, sem = (g.sync, "st") if 2 * n < len(spans) else (g.scalar, "st2")
-            q.wait_ge(S["ya%d" % n], P["arrive"][(core, "ya%d" % n)])
-            if core in comp and P["group"][core] == n:
-                q.wait_ge(S.vy, 6)
-            q.dma_start(T.y[:, a:b], T.yl[:, a:b]).then_inc(S[sem], 16)
-            count[sem] += 16
+        for q, sem, grp in ((g.sync, "st", near + far[0::2]), (g.scalar, "st2", far[1::2])):
+            for n in grp:
+                a, b = spans[n]
+                q.wait_ge(S["ya%d" % n], P["arrive"][(core, "ya%d" % n)])
+                if core in comp and P["group"][core] == n:
+                    q.wait_ge(S.vy, 6)
+                q.dma_start(T.y[:, a:b], T.yl[:, a:b]).then_inc(S[sem], 16)
+                count[sem] += 16
         g.sync.wait_ge(S.st, count["st"])
         g.scalar.wait_ge(S.st2, count["st2"])

from concourse.bass import DstId, RemoteDMATransfer
from concourse.mybir import AluOpType

NSIM = 80
C = 1024
ND = 2
WMAX = 96
WIDTH = {1: 96, 2: 64}
ON_CAP = 4
FEED_CAP = 8
DIAG = (1.0, -1.0, 5.0)
YL0 = 256

SCRATCH = {
    "xs": ("sbuf", [128, C], "bfloat16"),
    "yl": ("sbuf", [128, C], "bfloat16"),
    "xin": ("sbuf", [128, 6 * WMAX], "bfloat16"),
    "rl": ("sbuf", [128, 4 * WMAX], "bfloat16"),
    "nb": ("sbuf", [128, 15 * WMAX], "bfloat16"),
    "yo": ("sbuf", [128, 6 * WMAX], "bfloat16"),
    "zc": ("sbuf", [128, 128], "bfloat16"),
    "cm": ("sbuf", [128, 384], "bfloat16"),
    "xp0": ("psum", [128, 512], "float32"),
    "xp1": ("psum", [128, 512], "float32"),
    "xp2": ("psum", [128, 512], "float32"),
    "ac0": ("psum", [128, 512], "float32"),
    "ac1": ("psum", [128, 512], "float32"),
    "ac2": ("psum", [128, 512], "float32"),
    "ac3": ("psum", [128, 512], "float32"),
    "ac4": ("psum", [128, 512], "float32"),
}
SEMAPHORES = ["lda", "ldb", "st", "st2", "snt", "rarr", "ya0", "ya1", "ya2", "ya3",
              "xa0", "xa1", "xa2", "xa3", "xa4", "xa5",
              "cs", "ca", "cd", "pex", "pec", "pey", "v", "vy"]


def _bits(mask):
    return [e for e in range(mask.bit_length()) if (mask >> e) & 1]


def _give(pool, n, cap):
    per = 1
    while per * 2 * n <= len(pool) and per * 2 <= cap:
        per *= 2
    return [sum(1 << e for e in pool[t * per:(t + 1) * per]) for t in range(n)], per


def _call(topo, src, trs, cap=ON_CAP):
    off = [t for t in trs if topo.chip(t[0]) != topo.chip(src)]
    on = [t for t in trs if topo.chip(t[0]) == topo.chip(src)]
    out = []
    far = []
    if off:
        far = _bits(topo.mask(src, off[0][0]))
        masks, per = _give(far, len(off), len(far))
        out += [(t, m, per) for t, m in zip(off, masks)]
    if on:
        every = _bits(topo.mask(src, on[0][0]))
        some_far = [c for c in range(NSIM) if topo.chip(c) != topo.chip(src) and topo.may_write(src, c)]
        can_leave = _bits(topo.mask(src, some_far[0]))
        pool = [e for e in every if e not in can_leave] + [e for e in every if e in can_leave and e not in far]
        masks, per = _give(pool, len(on), cap)
        out += [(t, m, per) for t, m in zip(on, masks)]
    return out


def _by_width(trs):
    ws = sorted({t[5] for t in trs}, reverse=True)
    return [[t for t in trs if t[5] == w] for w in ws]


def _plan(T, topo):
    ranks = list(T.cores)
    chips = sorted({topo.chip(c) for c in ranks})
    all_chips = sorted({topo.chip(c) for c in range(NSIM)})

    def on_chip(ch):
        return [c for c in range(NSIM) if topo.chip(c) == ch]

    comp = []
    for ch in chips:
        for d in sorted({topo.die(c) for c in on_chip(ch)}):
            cand = [c for c in on_chip(ch) if topo.die(c) == d and all(c == r or topo.may_write(c, r) for r in ranks)]
            comp += sorted(cand, key=lambda c: (c not in ranks, c))[:ND]
    barred_at = {cc: [r for r in ranks if r != cc and not topo.may_write(r, cc)] for cc in comp}
    comp.sort(key=lambda c: (len(barred_at[c]), topo.chip(c), topo.die(c), c))
    shard = {}
    c0 = 0
    for cc in comp:
        shard[cc] = (c0, WIDTH[len(barred_at[cc])])
        c0 += shard[cc][1]
    assert c0 == C
    kinds = []
    for cc in comp:
        if topo.chip(cc) not in kinds:
            kinds.append(topo.chip(cc))
    group = {cc: kinds.index(topo.chip(cc)) for cc in comp}
    span = [(min(shard[cc][0] for cc in comp if group[cc] == n),
             max(shard[cc][0] + shard[cc][1] for cc in comp if group[cc] == n)) for n in range(len(kinds))]
    split = min(shard[cc][0] for cc in comp if shard[cc][1] != shard[comp[0]][1])

    feeds = {r: [] for r in ranks}
    now = {r: [] for r in ranks}
    later = {r: [] for r in ranks}
    relay, fill, asem, via, busy, thru = {}, {}, {}, set(), {}, {}

    def straight(lst, ri, cc):
        s0, w = shard[cc]
        lst.append((cc, "xs", s0, "xin", ri * w, w, "xa%d" % ri))
        asem[(cc, ri)] = "xa%d" % ri

    def room(q, w):
        o = fill.get(q, 0)
        fill[q] = o + w
        busy[q] = busy.get(q, 0) + 1
        return o

    def hand(ri, q, part):
        s0 = shard[part[0]][0]
        wt = sum(shard[cc][1] for cc in part)
        assert shard[part[-1]][0] + shard[part[-1]][1] - s0 == wt
        o = room(q, wt)
        feeds[ranks[ri]].append((q, "xs", s0, "rl", o, wt, "rarr"))
        for cc in part:
            w = shard[cc][1]
            relay.setdefault(q, []).append((cc, "rl", o + shard[cc][0] - s0, "xin", ri * w, w, "xa%d" % ri))
            asem[(cc, ri)] = "xa%d" % ri
            via.add((cc, ri))
            thru[(cc, ri)] = q

    def helpers(ch, part, src=None):
        return sorted([c for c in on_chip(ch) if c not in ranks and topo.die(c) == topo.die(part[0])
                       and all(topo.may_write(c, cc) for cc in part) and (src is None or topo.may_write(src, c))],
                      key=lambda c: (busy.get(c, 0), c not in comp, c))

    for ch in chips:
        rs = [ri for ri, r in enumerate(ranks) if topo.chip(r) == ch]
        cross = []
        for X in chips:
            tg = [cc for cc in comp if topo.chip(cc) == X]
            if X == ch or all(topo.may_write(ranks[ri], tg[0]) for ri in rs):
                for ri in rs:
                    for cc in tg:
                        if cc != ranks[ri]:
                            straight(now[ranks[ri]], ri, cc)
            else:
                cross.append(X)
        if len(cross) == 1:
            assert rs == list(range(rs[0], rs[0] + len(rs)))
            for cc in [c for c in comp if topo.chip(c) == cross[0]]:
                s0, w = shard[cc]
                q = helpers(ch, [cc])[0]
                o = room(q, w * len(rs))
                for n, ri in enumerate(rs):
                    feeds[ranks[ri]].append((q, "xs", s0, "rl", o + n * w, w, "rarr"))
                    asem[(cc, ri)] = "xa%d" % rs[0]
                    via.add((cc, ri))
                    thru[(cc, ri)] = q
                relay.setdefault(q, []).append((cc, "rl", o, "xin", rs[0] * w, w * len(rs), "xa%d" % rs[0]))
        elif cross:
            pending = []
            for X in cross:
                tg = [cc for cc in comp if topo.chip(cc) == X]
                for d in sorted({topo.die(cc) for cc in tg}):
                    part = [cc for cc in tg if topo.die(cc) == d]
                    for ri in rs:
                        r = ranks[ri]
                        if not topo.may_write(r, part[0]):
                            if topo.mates(ch, X):
                                hand(ri, helpers(ch, part)[0], part)
                            else:
                                Z = [z for z in all_chips if topo.mates(z, X)][0]
                                hand(ri, helpers(Z, part, r)[0], part)
                        elif topo.mates(ch, X):
                            for cc in part:
                                straight(now[r], ri, cc)
                        else:
                            pending.append((ri, part))
            for ri, part in pending:
                free = [c for c in helpers(ch, part) if c not in busy]
                for Z in [z for z in all_chips if topo.mates(z, topo.chip(part[0]))]:
                    free += [c for c in helpers(Z, part, ranks[ri]) if c not in busy]
                if free:
                    hand(ri, free[0], part)
                else:
                    for cc in part:
                        straight(later[ranks[ri]], ri, cc)

    calls = {}
    for r in ranks:
        calls[r] = [("scatter", _call(topo, r, trs, FEED_CAP)) for trs in _by_width(feeds[r])]
        calls[r] += [("scatter", _call(topo, r, trs)) for trs in _by_width(now[r]) + _by_width(later[r])]
    for q, trs in relay.items():
        calls.setdefault(q, []).extend(("relay", _call(topo, q, grp)) for grp in _by_width(trs))

    how, fed = {}, {}
    for src, lst in calls.items():
        for ci, (_, call) in enumerate(lst):
            for t, m, per in call:
                how[(t[0], t[6])] = (ci, -per)
                if src in ranks and t[3] == "rl":
                    fed[(src, t[0])] = -per
    order = {}
    for cc in comp:
        order[cc] = sorted(range(len(ranks)), key=lambda ri: (
            (cc, ri) in via, topo.chip(ranks[ri]) != topo.chip(cc), ranks[ri] != cc,
            how.get((cc, asem.get((cc, ri))), (0, 0)), fed.get((ranks[ri], thru.get((cc, ri))), 0), ri))
    nlate = {cc: len([ri for ri in range(len(ranks)) if (cc, ri) in via]) for cc in comp}

    finals = {}
    for cc in comp:
        s0, w = shard[cc]
        far = [ri for ri in order[cc][:5] if topo.chip(ranks[ri]) != topo.chip(cc)] + [order[cc][5]]
        near = [ri for ri in order[cc][:5] if topo.chip(ranks[ri]) == topo.chip(cc) and ranks[ri] != cc]
        own = [ri for ri in order[cc][:5] if ranks[ri] == cc]
        finals[cc] = (far, near, own)
        for name, grp in (("far", far), ("near", near)):
            trs = [(ranks[ri], "yo", ri * WMAX, "yl", s0, w, "ya%d" % group[cc]) for ri in grp]
            calls.setdefault(cc, []).append((name, _call(topo, cc, trs)))

    warm = {}
    for ch in chips:
        R = sorted([c for c in comp if topo.chip(c) == ch], key=lambda c: (c in ranks, c))
        E = [c for c in sorted(calls) if c not in comp and
             (topo.chip(c) == ch if c in ranks else topo.chip(calls[c][0][1][0][0][0]) == ch)]
        E.sort(key=lambda c: (c not in ranks, c))
        kind = {c: n % 3 for n, c in enumerate(R)}
        kind.update({c: 1 + n % 2 for n, c in enumerate(E)})
        gets = {c: [] for c in R + E}
        for c in R:
            for k in range(3):
                if kind[c] != k:
                    cand = [q for q in R + E if kind[q] == k and q != c and topo.may_write(q, c)]
                    gets[min(cand, key=lambda q: (len(gets[q]), q in ranks, q))].append(c)
        for q in R + E:
            assert gets[q]
            m = topo.mask(q, gets[q][0])
            assert all(topo.mask(q, c) == m for c in gets[q])
            warm[q] = (kind[q], gets[q], m, len(_bits(m)))

    arrive = {}
    sent = {}
    for q, (k, ds, m, per) in warm.items():
        sent[q] = per
        for c in ds:
            arrive[(c, "cd")] = arrive.get((c, "cd"), 0) + per
    for src, lst in calls.items():
        for _, call in lst:
            for t, m, per in call:
                arrive[(t[0], t[6])] = arrive.get((t[0], t[6]), 0) + per
                sent[src] = sent.get(src, 0) + per
    return dict(ranks=ranks, comp=comp, shard=shard, order=order, calls=calls, finals=finals, arrive=arrive,
                sent=sent, warm=warm, nlate=nlate, asem=asem, group=group, span=span, split=split, gchip=kinds)


def _issue(g, T, topo, call):
    trs = []
    for t, m, per in call:
        dst, sb, s0, db, d0, w, sem = t
        rid, pid, _se = topo.addr(dst)
        trs.append(RemoteDMATransfer(dst_ids=[DstId(rid=rid, pnc=pid)], dma_engine_mask=m, remote_sem=T.sem[sem],
                                     src=T[sb][:, s0:s0 + w], dst=T[db][:, d0:d0 + w]))
    g.remote_dma_fused(trs, local_sem=T.sem.snt)


def _compute(g, core, T, P):
    S = T.sem
    ranks = P["ranks"]
    s0, w = P["shard"][core]
    order = P["order"][core]
    far, near, own = P["finals"][core]
    pe, ve = g.tensor, g.vector

    eye, neg, five = T.cm[:, 0:128], T.cm[:, 128:256], T.cm[:, 256:384]

    def X(k):
        ri = order[k]
        if ranks[ri] == core:
            return T.xs[:, s0:s0 + w]
        return T.xin[:, ri * w:ri * w + w]

    def wait_x(q, k):
        ri = order[k]
        if ranks[ri] == core:
            q.wait_ge(S.lda if s0 < P["split"] else S.ldb, 16)
        else:
            name = P["asem"][(core, ri)]
            q.wait_ge(S[name], P["arrive"][(core, name)])

    xpb = [T.xp0, T.xp1, T.xp2]
    acb = [T.ac0, T.ac1, T.ac2, T.ac3, T.ac4]

    def XP(i):
        return xpb[i // 2][:, (i % 2) * WMAX:(i % 2) * WMAX + w]

    def need_pex(i):
        return min(5, (i // 2) * 2 + 2)

    yL = T.xp2[:, YL0:YL0 + w]
    pairs = [(i, k) for k in range(1, 5) for i in range(k)] + [(i, 5) for i in (4, 0, 1, 2, 3)]
    pos = {p: n for n, p in enumerate(pairs)}

    def NB(p):
        return T.nb[:, pos[p] * WMAX:pos[p] * WMAX + w]

    pe.wait_ge(S.ca, 1)
    pe.wait_ge(S.cd, P["arrive"][(core, "cd")])

    def bring(k):
        wait_x(pe, k)
        pe.matmul(XP(k), eye, X(k), start=True, stop=True).then_inc(S.pex, 1)

    def open_acc(k):
        pe.matmul(acb[k][:, 0:w], five, X(k), start=True, stop=False)

    def add_pairs(k):
        for i in range(k):
            pe.wait_ge(S.v, pos[(i, k)] + 1)
            m = pe.matmul(acb[i][:, 0:w], neg, NB((i, k)), start=False, stop=(k == 4))
            if k == 4:
                m.then_inc(S.pec, 1)
            m = pe.matmul(acb[k][:, 0:w], neg, NB((i, k)), start=False, stop=(k == 4 and i == 3))
            if k == 4 and i == 3:
                m.then_inc(S.pec, 1)

    ne = min(6 - P["nlate"][core], 5)
    for k in range(ne):
        bring(k)
    for k in range(ne):
        open_acc(k)
    for k in range(1, ne):
        add_pairs(k)
    for k in range(ne, 5):
        bring(k)
        open_acc(k)
        add_pairs(k)
    wait_x(pe, 5)
    pe.wait_ge(S.v, pos[(4, 5)] + 1)
    pe.matmul(yL, five, X(5), start=True, stop=False)
    for n, i in enumerate((4, 0, 1, 2, 3)):
        pe.wait_ge(S.v, pos[(i, 5)] + 1)
        m = pe.matmul(yL, neg, NB((i, 5)), start=False, stop=(n == 4))
        if n == 4:
            m.then_inc(S.pey, 1)

    seen = -1
    for (i, k) in pairs:
        if k != seen:
            wait_x(ve, k)
            seen = k
        ve.wait_ge(S.pex, need_pex(i))
        ve.tensor_tensor(NB((i, k)), XP(i), X(k), AluOpType.min).then_inc(S.v, 1)
    ve.wait_ge(S.v, len(pairs))
    for ri in far + near + own:
        out = T.yl[:, s0:s0 + w] if ranks[ri] == core else T.yo[:, ri * WMAX:ri * WMAX + w]
        i = order.index(ri)
        if i == 5:
            ve.wait_ge(S.pey, 1)
            ve.tensor_copy(out, yL).then_inc(S.vy, 1)
        else:
            ve.wait_ge(S.pec, i + 1)
            ve.tensor_tensor(out, acb[i][:, 0:w], NB((i, 5)), AluOpType.subtract).then_inc(S.vy, 1)
    ve.wait_ge(S.pec, 5)


def rank_program(g, core, T, topo):
    P = _plan(T, topo)
    S = T.sem
    ranks, comp = P["ranks"], P["comp"]
    if core not in P["calls"]:
        return
    is_rank = core in ranks

    split = P["split"]
    if is_rank:
        a_first = P["calls"][core][0][1][0][0][2] < split
        qa, qb = (g.sync, g.scalar) if a_first else (g.scalar, g.sync)
        for first in (True, False):
            if first == a_first:
                qa.dma_start(T.xs[:, 0:split], T.x[:, 0:split]).then_inc(S.lda, 16)
            else:
                qb.dma_start(T.xs[:, split:C], T.x[:, split:C]).then_inc(S.ldb, 16)

    k, takers, m, per = P["warm"][core]
    part = T.cm[:, k * 128:(k + 1) * 128]
    g.vector.memset(T.zc[:, :], DIAG[k]).then_inc(S.cs, 1)
    g.wait_ge(S.cs, 1)
    g.affine_select(part, T.zc[:, :], [[-1, 128]], AluOpType.is_equal, 0.0, 0, 1).then_inc(S.ca, 1)
    g.wait_ge(S.ca, 1)
    ids = [DstId(rid=topo.addr(c)[0], pnc=topo.addr(c)[1]) for c in takers]
    g.remote_dma_fused([RemoteDMATransfer(dst_ids=ids, dma_engine_mask=m, remote_sem=S.cd, srcs=[part],
                                          dsts=[part for c in takers])], local_sem=S.snt)

    if core in comp:
        _compute(g, core, T, P)

    done = 0
    for stage, call in P["calls"][core]:
        if not call:
            continue
        if stage == "scatter":
            g.wait_ge(S.lda if call[0][0][2] < split else S.ldb, 16)
        elif stage == "relay":
            g.wait_ge(S.rarr, P["arrive"][(core, "rarr")])
        else:
            done += len(call)
            g.wait_ge(S.vy, done)
        _issue(g, T, topo, call)
    g.wait_ge(S.snt, P["sent"][core])

    if is_rank:
        spans = P["span"]
        near = [n for n in range(len(spans)) if P["gchip"][n] == topo.chip(core)]
        far = [n for n in range(len(spans)) if n not in near]
        count = {"st": 0, "st2": 0}
        for q, sem, grp in ((g.sync, "st", near + far[0::2]), (g.scalar, "st2", far[1::2])):
            for n in grp:
                a, b = spans[n]
                q.wait_ge(S["ya%d" % n], P["arrive"][(core, "ya%d" % n)])
                if core in comp and P["group"][core] == n:
                    q.wait_ge(S.vy, 6)
                q.dma_start(T.y[:, a:b], T.yl[:, a:b]).then_inc(S[sem], 16)
                count[sem] += 16
        g.sync.wait_ge(S.st, count["st"])
        g.scalar.wait_ge(S.st2, count["st2"])
